import numpy as np, ml_dtypes
CORES = [2,34,66,98,130,162,194,226,258,290,322,354,386,418,450,482]
N = 16
QP = 128
def setup_inputs(rng):
    m = 150 * rng.standard_normal((1, QP, 1), dtype=np.float32) + 3 * rng.standard_normal((N, QP, 1), dtype=np.float32)
    m = (m + rng.uniform(100, 300, (1, QP, 1)) * (rng.random((1, QP, 1)) < 0.7) * (rng.random((N, QP, 1)) < 0.5)).astype(np.float32)
    l = 20 * (1 + np.abs(rng.standard_normal((N, QP, 1), dtype=np.float32)))
    return {"o": (l * rng.standard_normal((N, QP, 128), dtype=np.float32) / 4).astype(ml_dtypes.bfloat16), "ml": np.concatenate([m, l], axis=2)}
def setup_inputs_big(rng):
    d = setup_inputs(rng)
    for k in ("o",): d[k] = (d[k].astype(np.float32) * 1048576.0).astype(d[k].dtype)
    return d
def setup_inputs_small(rng):
    d = setup_inputs(rng)
    for k in ("o",): d[k] = (d[k].astype(np.float32) * (1 / 1048576.0)).astype(d[k].dtype)
    return d
def setup_inputs_apart(rng):
    d = setup_inputs(rng)
    f = (10.0 ** rng.permutation(np.linspace(-1.5, 1.5, N))).astype(np.float32).reshape(N, 1, 1)
    for k in ("o",): d[k] = (d[k].astype(np.float32) * f).astype(d[k].dtype)
    return d
def reference(o, ml):
    O, ML = o.astype(np.float64), ml.astype(np.float64)
    m, l = ML[:, :, 0:1], ML[:, :, 1:2]
    f = np.exp(m - m.max(axis=0))
    y = ((f * O).sum(axis=0) / (f * l).sum(axis=0)).astype(ml_dtypes.bfloat16)
    return {"y": np.stack([y[QP // N * r:QP // N * (r + 1)] for r in range(N)])}

@@ -1,0 +1,189 @@
+from concourse.bass import DstId, RemoteDMATransfer
+from concourse.mybir import AluOpType, AxisListType, ActivationFunctionType
+
+QR = 8
+D = 128
+ND = 12
+PD = ND * QR
+PL = 5 * QR
+BIG = 1.0e4
+
+SCRATCH = {
+    "stage_o": ("dram", [16, 128, 8], "bfloat16"),
+    "stage_ml": ("dram", [128, 4], "float32"),
+    "land_o": ("dram", [16, 128, 8], "bfloat16"),
+    "land_ml": ("dram", [16, 128, 4], "float32"),
+    "relay_o": ("dram", [4, 128, 8], "bfloat16"),
+    "xd": ("sbuf", [128, 136], "bfloat16"),
+    "xl": ("sbuf", [128, 136], "bfloat16"),
+    "mld": ("sbuf", [128, 2], "float32"),
+    "mll": ("sbuf", [128, 2], "float32"),
+    "ones": ("sbuf", [128, PD], "float32"),
+    "st": ("sbuf", [128, PD], "float32"),
+    "b": ("sbuf", [128, PD], "float32"),
+    "mask": ("sbuf", [128, ND], "float32"),
+    "nm": ("sbuf", [128, 40], "float32"),
+    "zd": ("sbuf", [128, ND], "float32"),
+    "zl": ("sbuf", [128, 8], "float32"),
+    "gd": ("sbuf", [128, 40], "float32"),
+    "gl": ("sbuf", [128, 8], "float32"),
+    "wd": ("sbuf", [128, 40], "bfloat16"),
+    "wl": ("sbuf", [128, 8], "bfloat16"),
+    "negm1": ("sbuf", [128, 1], "float32"),
+    "negm": ("sbuf", [128, 1], "float32"),
+    "rden": ("sbuf", [128, 1], "float32"),
+    "ysb": ("sbuf", [128, D], "bfloat16"),
+    "p_b": ("psum", [128, 512], "float32"),
+    "p_mf1": ("psum", [128, 512], "float32"),
+    "p_acc": ("psum", [128, 512], "float32"),
+    "p_mf2": ("psum", [128, 512], "float32"),
+    "p_out": ("psum", [128, 512], "float32"),
+}
+SEMAPHORES = (["st_o", "st_ml", "own_o", "own_ml", "ld_mld", "ld_xd", "ld_mll", "ld_xl", "stored",
+               "rin", "din_o", "late_o", "late_ml", "sent", "ml_h0", "ml_h1", "ml_h2", "ml_h3"]
+              + ["c%d" % i for i in range(32)])
+
+
+def _order(d, cores, topo):
+    same = [c for c in cores if c != d and topo.host(c) == topo.host(d)]
+    peer = [c for c in cores if topo.host(c) != topo.host(d) and topo.rack(topo.host(c)) == topo.rack(topo.host(d))]
+    far = [c for c in cores if topo.rack(topo.host(c)) != topo.rack(topo.host(d))]
+    cable = [c for c in far if topo.may_write(c, d)]
+    diag = [c for c in far if not topo.may_write(c, d)]
+    return [d] + same + peer + cable + diag, same, peer, cable, diag
+
+
+def rank_program(g, core, T, topo):
+    rank = T.rank_of(core)
+    if rank is None:
+        return
+    cores = list(T.cores)
+    S = T.sem
+    V, PE, ACT, SY = g.vector, g.tensor, g.scalar, g.sync
+    mult, add, mx = AluOpType.mult, AluOpType.add, AluOpType.max
+    _, same, peer, cable, diag = _order(core, cores, topo)
+    slot = lambda dst, src: _order(dst, cores, topo)[0].index(src)
+    nsem = [0]
+
+    def mark(ins):
+        s = S["c%d" % nsem[0]]
+        nsem[0] += 1
+        ins.then_inc(s, 1)
+        return s
+
+    def did(dst):
+        rid, pid = topo.addr(dst, core)
+        return DstId(rid=rid, pnc=pid)
+
+    def fused(items):
+        ok = ~0
+        for _, dl, _ in items:
+            for dst, _ in dl:
+                ok &= topo.mask(core, dst)
+        eng = [1 << i for i in range(16) if (ok >> i) & 1]
+        g.remote_dma_fused([RemoteDMATransfer(dst_ids=[did(dst) for dst, _ in dl], dma_engine_mask=eng[i], remote_sem=sem,
+                                              srcs=[src], dsts=[ap for _, ap in dl])
+                            for i, (src, dl, sem) in enumerate(items)], local_sem=S.sent)
+        return len(items)
+
+    SY.dma_start(T.stage_o[:], T.o[:]).then_inc(S.st_o, 16)
+    ACT.dma_start(T.stage_ml[0:64, :], T.ml[:]).then_inc(S.st_ml, 16)
+    ACT.dma_start(T.stage_ml[64:128, :], T.ml[:]).then_inc(S.st_ml, 16)
+    SY.dma_start(T.xd[0:QR, 0:D], T.o[QR * rank:QR * rank + QR, :]).then_inc(S.own_o, 16)
+    ACT.dma_start(T.mld[0:QR, 0:2], T.ml[QR * rank:QR * rank + QR, :]).then_inc(S.own_ml, 16)
+
+    s_ones = mark(V.memset(T.ones[0:QR, 0:PD], 1.0))
+    s_mk0 = mark(V.memset(T.mask[0:PD, 0:ND], 1.0))
+    s_nm0 = mark(V.memset(T.nm[0:PD, 0:32], -BIG))
+    g.wait_ge(s_ones, 1)
+    s_st = mark(g.affine_select(T.st[0:QR, 0:PD], T.ones[0:QR, 0:PD], [[0, ND], [-1, QR]], AluOpType.is_equal, 0.0, 0, 1))
+    g.wait_ge(s_mk0, 1)
+    s_mk1 = mark(g.affine_select(T.mask[0:PD, 0:ND], T.mask[0:PD, 0:ND], [[-QR, ND]], AluOpType.is_ge, 0.0, 0, 1))
+    g.wait_ge(s_mk1, 1)
+    s_mk = mark(g.affine_select(T.mask[0:PD, 0:ND], T.mask[0:PD, 0:ND], [[QR, ND]], AluOpType.is_ge, 0.0, QR - 1, -1))
+    PE.wait_ge(s_st, 1)
+    s_pb = mark(PE.matmul(T.p_b[0:PD, 0:PD], T.st[0:QR, 0:PD], T.st[0:QR, 0:PD], True, True))
+    V.wait_ge(s_pb, 1)
+    s_b = mark(V.tensor_copy(T.b[0:PD, 0:PD], T.p_b[0:PD, 0:PD]))
+    s_nm1 = mark(V.tensor_scalar(T.nm[0:PD, 32:40], T.p_b[0:PD, 0:QR], -1.0, BIG, add, mult))
+
+    mysem = S["ml_h%d" % topo.host(core)]
+    relay_of = {d: [r for r in peer if topo.chip(r) == topo.chip(d) and topo.may_write(r, d)][0] for d in diag}
+    items = [(T.stage_o[T.rank_of(d)], [(relay_of[d], T.relay_o[slot(relay_of[d], core) - 4])], S.rin) for d in diag]
+    items.append((T.stage_ml[:], [(d, T.land_ml[slot(d, core)]) for d in peer + cable + same], mysem))
+    items += [(T.stage_o[T.rank_of(d)], [(d, T.land_o[slot(d, core)])], S.din_o) for d in cable + peer + same]
+    g.wait_ge(S.st_o, 16)
+    g.wait_ge(S.st_ml, 32)
+    sent = fused(items[0:8])
+    sent += fused(items[8:16])
+
+    nxt = [d for d in cable if topo.chip(d) == topo.chip(core)][0]
+    peersem = S["ml_h%d" % topo.host(peer[0])]
+    g.wait_ge(S.rin, 4)
+    g.wait_ge(peersem, 4)
+    sent += fused([(T.land_ml[4 + k], [(nxt, T.land_ml[slot(nxt, peer[k])])], S.late_ml) for k in range(4)]
+                  + [(T.relay_o[k], [(nxt, T.land_o[slot(nxt, peer[k])])], S.late_o) for k in range(4)])
+
+    r4 = 4 * rank
+    SY.wait_ge(mysem, len(same))
+    SY.wait_ge(peersem, 4)
+    SY.wait_ge(S["ml_h%d" % topo.host(cable[0])], 4)
+    SY.dma_start(T.mld[QR:PD, 0:2], T.land_ml[1:ND, r4:r4 + 4, :]).then_inc(S.ld_mld, 16)
+    SY.wait_ge(S.din_o, ND - 1)
+    SY.dma_start(T.xd[QR:PD, 0:D], T.land_o[1:ND]).then_inc(S.ld_xd, 16)
+    SY.wait_ge(S.late_ml, 4)
+    SY.dma_start(T.mll[0:32, 0:2], T.land_ml[ND:16, r4:r4 + 4, :]).then_inc(S.ld_mll, 16)
+    SY.wait_ge(S.late_o, 4)
+    SY.dma_start(T.xl[0:32, 0:D], T.land_o[ND:16]).then_inc(S.ld_xl, 16)
+
+    V.wait_ge(S.own_ml, 16)
+    V.wait_ge(S.ld_mld, 16)
+    V.wait_ge(s_mk, 1)
+    s_zd = mark(V.tensor_scalar(T.zd[0:PD, 0:ND], T.mask[0:PD, 0:ND], T.mld[0:PD, 0:1], None, mult))
+    V.wait_ge(s_nm0, 1)
+    V.wait_ge(s_nm1, 1)
+    s_gd = mark(V.tensor_scalar(T.gd[0:PD, 0:40], T.nm[0:PD, 0:40], T.mld[0:PD, 0:1], None, add))
+    s_ld = mark(V.tensor_copy(T.xd[0:PD, D:D + 1], T.mld[0:PD, 1:2]))
+    PE.wait_ge(s_b, 1)
+    PE.wait_ge(s_zd, 1)
+    s_mf1 = mark(PE.matmul(T.p_mf1[0:PD, 0:ND], T.b[0:PD, 0:PD], T.zd[0:PD, 0:ND], True, True))
+    V.wait_ge(s_mf1, 1)
+    s_negm1 = mark(V.tensor_reduce(T.negm1[0:PD, 0:1], T.p_mf1[0:PD, 0:ND], AxisListType.X, mx, negate=True))
+    s_m1 = mark(V.tensor_reduce(T.mll[32:40, 0:1], T.p_mf1[32:40, 0:ND], AxisListType.X, mx))
+    ACT.wait_ge(s_gd, 1)
+    ACT.wait_ge(s_negm1, 1)
+    s_wd = mark(ACT.activation(T.wd[0:PD, 0:40], T.gd[0:PD, 0:40], ActivationFunctionType.Exp, bias=T.negm1[0:PD, 0:1]))
+    PE.wait_ge(s_wd, 1)
+    PE.wait_ge(s_ld, 1)
+    PE.wait_ge(S.own_o, 16)
+    PE.wait_ge(S.ld_xd, 16)
+    s_acc = mark(PE.matmul(T.p_acc[0:PL, 0:D + 1], T.wd[0:PD, 0:40], T.xd[0:PD, 0:D + 1], True, True))
+    ACT.wait_ge(s_acc, 1)
+    s_x5 = mark(ACT.activation(T.xl[32:40, 0:D + 1], T.p_acc[32:40, 0:D + 1], ActivationFunctionType.Copy))
+
+    V.wait_ge(S.ld_mll, 16)
+    V.wait_ge(s_m1, 1)
+    s_zl = mark(V.tensor_scalar(T.zl[0:PL, 0:5], T.mask[0:PL, 0:5], T.mll[0:PL, 0:1], None, mult))
+    s_gl = mark(V.tensor_scalar(T.gl[0:PL, 0:QR], T.nm[0:PL, 32:40], T.mll[0:PL, 0:1], None, add))
+    s_ll = mark(V.tensor_copy(T.xl[0:32, D:D + 1], T.mll[0:32, 1:2]))
+    PE.wait_ge(s_zl, 1)
+    s_mf2 = mark(PE.matmul(T.p_mf2[0:PL, 0:5], T.b[0:PL, 0:PL], T.zl[0:PL, 0:5], True, True))
+    V.wait_ge(s_mf2, 1)
+    s_negm = mark(V.tensor_reduce(T.negm[0:PL, 0:1], T.p_mf2[0:PL, 0:5], AxisListType.X, mx, negate=True))
+    ACT.wait_ge(s_gl, 1)
+    ACT.wait_ge(s_negm, 1)
+    s_wl = mark(ACT.activation(T.wl[0:PL, 0:QR], T.gl[0:PL, 0:QR], ActivationFunctionType.Exp, bias=T.negm[0:PL, 0:1]))
+    PE.wait_ge(s_wl, 1)
+    PE.wait_ge(s_x5, 1)
+    PE.wait_ge(s_ll, 1)
+    PE.wait_ge(S.ld_xl, 16)
+    s_out = mark(PE.matmul(T.p_out[0:QR, 0:D + 1], T.wl[0:PL, 0:QR], T.xl[0:PL, 0:D + 1], True, True))
+    V.wait_ge(s_out, 1)
+    s_rd = mark(V.reciprocal(T.rden[0:QR, 0:1], T.p_out[0:QR, D:D + 1]))
+    V.wait_ge(s_rd, 1)
+    s_y = mark(V.tensor_scalar(T.ysb[0:QR, 0:D], T.p_out[0:QR, 0:D], T.rden[0:QR, 0:1], None, mult))
+    SY.wait_ge(s_y, 1)
+    SY.dma_start(T.y[:], T.ysb[0:QR, 0:D]).then_inc(S.stored, 16)
+
+    g.wait_ge(S.sent, sent)
+    g.wait_ge(S.stored, 16)

@@ -3,9 +3,10 @@ from concourse.mybir import AluOpType, AxisListType, ActivationFunctionType
 
 QR = 8
 D = 128
+NS = 16
 ND = 12
+P = NS * QR
 PD = ND * QR
-PL = 5 * QR
 BIG = 1.0e4
 
 SCRATCH = {
@@ -14,34 +15,27 @@ SCRATCH = {
     "land_o": ("dram", [16, 128, 8], "bfloat16"),
     "land_ml": ("dram", [16, 128, 4], "float32"),
     "relay_o": ("dram", [4, 128, 8], "bfloat16"),
-    "xd": ("sbuf", [128, 136], "bfloat16"),
-    "xl": ("sbuf", [128, 136], "bfloat16"),
-    "mld": ("sbuf", [128, 2], "float32"),
-    "mll": ("sbuf", [128, 2], "float32"),
-    "ones": ("sbuf", [128, PD], "float32"),
-    "st": ("sbuf", [128, PD], "float32"),
-    "b": ("sbuf", [128, PD], "float32"),
-    "mask": ("sbuf", [128, ND], "float32"),
-    "nm": ("sbuf", [128, 40], "float32"),
-    "zd": ("sbuf", [128, ND], "float32"),
-    "zl": ("sbuf", [128, 8], "float32"),
-    "gd": ("sbuf", [128, 40], "float32"),
-    "gl": ("sbuf", [128, 8], "float32"),
-    "wd": ("sbuf", [128, 40], "bfloat16"),
-    "wl": ("sbuf", [128, 8], "bfloat16"),
-    "negm1": ("sbuf", [128, 1], "float32"),
+    "x": ("sbuf", [128, 136], "bfloat16"),
+    "ml_sb": ("sbuf", [128, 2], "float32"),
+    "ones": ("sbuf", [128, P], "float32"),
+    "st": ("sbuf", [128, P], "float32"),
+    "b": ("sbuf", [128, P], "bfloat16"),
+    "mask": ("sbuf", [128, NS], "float32"),
+    "nm": ("sbuf", [128, QR], "float32"),
+    "z": ("sbuf", [128, NS], "bfloat16"),
+    "gm": ("sbuf", [128, QR], "float32"),
+    "w": ("sbuf", [128, QR], "bfloat16"),
     "negm": ("sbuf", [128, 1], "float32"),
     "rden": ("sbuf", [128, 1], "float32"),
     "ysb": ("sbuf", [128, D], "bfloat16"),
     "p_b": ("psum", [128, 512], "float32"),
-    "p_mf1": ("psum", [128, 512], "float32"),
-    "p_acc": ("psum", [128, 512], "float32"),
-    "p_mf2": ("psum", [128, 512], "float32"),
+    "p_mf": ("psum", [128, 512], "float32"),
+    "p_den": ("psum", [128, 512], "float32"),
     "p_out": ("psum", [128, 512], "float32"),
 }
 SEMAPHORES = (["st_o", "st_ml", "own_o", "own_ml", "ld_mld", "ld_xd", "ld_mll", "ld_xl", "stored",
                "rin", "din_o", "late_o", "late_ml", "sent", "ml_h0", "ml_h1", "ml_h2", "ml_h3"]
-              + ["c%d" % i for i in range(32)])
+              + ["c%d" % i for i in range(24)])
 
 
 def _order(d, cores, topo):
@@ -61,6 +55,7 @@ def rank_program(g, core, T, topo):
     S = T.sem
     V, PE, ACT, SY = g.vector, g.tensor, g.scalar, g.sync
     mult, add, mx = AluOpType.mult, AluOpType.add, AluOpType.max
+    Exp = ActivationFunctionType.Exp
     _, same, peer, cable, diag = _order(core, cores, topo)
     slot = lambda dst, src: _order(dst, cores, topo)[0].index(src)
     nsem = [0]
@@ -89,33 +84,36 @@ def rank_program(g, core, T, topo):
     SY.dma_start(T.stage_o[:], T.o[:]).then_inc(S.st_o, 16)
     ACT.dma_start(T.stage_ml[0:64, :], T.ml[:]).then_inc(S.st_ml, 16)
     ACT.dma_start(T.stage_ml[64:128, :], T.ml[:]).then_inc(S.st_ml, 16)
-    SY.dma_start(T.xd[0:QR, 0:D], T.o[QR * rank:QR * rank + QR, :]).then_inc(S.own_o, 16)
-    ACT.dma_start(T.mld[0:QR, 0:2], T.ml[QR * rank:QR * rank + QR, :]).then_inc(S.own_ml, 16)
+    SY.dma_start(T.x[0:QR, 0:D], T.o[QR * rank:QR * rank + QR, :]).then_inc(S.own_o, 16)
+    ACT.dma_start(T.ml_sb[0:QR, 0:2], T.ml[QR * rank:QR * rank + QR, :]).then_inc(S.own_ml, 16)
 
-    s_ones = mark(V.memset(T.ones[0:QR, 0:PD], 1.0))
-    s_mk0 = mark(V.memset(T.mask[0:PD, 0:ND], 1.0))
-    s_nm0 = mark(V.memset(T.nm[0:PD, 0:32], -BIG))
+    s_ones = mark(V.memset(T.ones[0:QR, 0:P], 1.0))
+    s_mk0 = mark(V.memset(T.mask[0:P, 0:NS], 1.0))
     g.wait_ge(s_ones, 1)
-    s_st = mark(g.affine_select(T.st[0:QR, 0:PD], T.ones[0:QR, 0:PD], [[0, ND], [-1, QR]], AluOpType.is_equal, 0.0, 0, 1))
+    s_st = mark(g.affine_select(T.st[0:QR, 0:P], T.ones[0:QR, 0:P], [[0, NS], [-1, QR]], AluOpType.is_equal, 0.0, 0, 1))
     g.wait_ge(s_mk0, 1)
-    s_mk1 = mark(g.affine_select(T.mask[0:PD, 0:ND], T.mask[0:PD, 0:ND], [[-QR, ND]], AluOpType.is_ge, 0.0, 0, 1))
+    s_mk1 = mark(g.affine_select(T.mask[0:P, 0:NS], T.mask[0:P, 0:NS], [[-QR, NS]], AluOpType.is_ge, 0.0, 0, 1))
     g.wait_ge(s_mk1, 1)
-    s_mk = mark(g.affine_select(T.mask[0:PD, 0:ND], T.mask[0:PD, 0:ND], [[QR, ND]], AluOpType.is_ge, 0.0, QR - 1, -1))
+    s_mk = mark(g.affine_select(T.mask[0:P, 0:NS], T.mask[0:P, 0:NS], [[QR, NS]], AluOpType.is_ge, 0.0, QR - 1, -1))
     PE.wait_ge(s_st, 1)
-    s_pb = mark(PE.matmul(T.p_b[0:PD, 0:PD], T.st[0:QR, 0:PD], T.st[0:QR, 0:PD], True, True))
+    s_pb = mark(PE.matmul(T.p_b[0:P, 0:P], T.st[0:QR, 0:P], T.st[0:QR, 0:P], True, True))
     V.wait_ge(s_pb, 1)
-    s_b = mark(V.tensor_copy(T.b[0:PD, 0:PD], T.p_b[0:PD, 0:PD]))
-    s_nm1 = mark(V.tensor_scalar(T.nm[0:PD, 32:40], T.p_b[0:PD, 0:QR], -1.0, BIG, add, mult))
+    s_nm = mark(V.tensor_scalar(T.nm[0:P, 0:QR], T.p_b[0:P, 0:QR], -1.0, BIG, add, mult))
+    ACT.wait_ge(s_nm, 1)
+    s_b = mark(ACT.activation(T.b[0:P, 0:P], T.p_b[0:P, 0:P], Exp, bias=-BIG, scale=BIG))
 
     mysem = S["ml_h%d" % topo.host(core)]
     relay_of = {d: [r for r in peer if topo.chip(r) == topo.chip(d) and topo.may_write(r, d)][0] for d in diag}
-    items = [(T.stage_o[T.rank_of(d)], [(relay_of[d], T.relay_o[slot(relay_of[d], core) - 4])], S.rin) for d in diag]
-    items.append((T.stage_ml[:], [(d, T.land_ml[slot(d, core)]) for d in peer + cable + same], mysem))
-    items += [(T.stage_o[T.rank_of(d)], [(d, T.land_o[slot(d, core)])], S.din_o) for d in cable + peer + same]
+    ml_to = lambda ds: (T.stage_ml[:], [(d, T.land_ml[slot(d, core)]) for d in ds], mysem)
+    first = [ml_to([d]) for d in peer]
+    first += [(T.stage_o[T.rank_of(d)], [(relay_of[d], T.relay_o[slot(relay_of[d], core) - 4])], S.rin) for d in diag]
+    rest = [ml_to(cable), ml_to(same)]
+    rest += [(T.stage_o[T.rank_of(d)], [(d, T.land_o[slot(d, core)])], S.din_o) for d in cable + peer + same]
     g.wait_ge(S.st_o, 16)
     g.wait_ge(S.st_ml, 32)
-    sent = fused(items[0:8])
-    sent += fused(items[8:16])
+    sent = fused(first)
+    sent += fused(rest[0:8])
+    sent += fused(rest[8:])
 
     nxt = [d for d in cable if topo.chip(d) == topo.chip(core)][0]
     peersem = S["ml_h%d" % topo.host(peer[0])]
@@ -128,59 +126,41 @@ def rank_program(g, core, T, topo):
     SY.wait_ge(mysem, len(same))
     SY.wait_ge(peersem, 4)
     SY.wait_ge(S["ml_h%d" % topo.host(cable[0])], 4)
-    SY.dma_start(T.mld[QR:PD, 0:2], T.land_ml[1:ND, r4:r4 + 4, :]).then_inc(S.ld_mld, 16)
+    SY.dma_start(T.ml_sb[QR:PD, 0:2], T.land_ml[1:ND, r4:r4 + 4, :]).then_inc(S.ld_mld, 16)
     SY.wait_ge(S.din_o, ND - 1)
-    SY.dma_start(T.xd[QR:PD, 0:D], T.land_o[1:ND]).then_inc(S.ld_xd, 16)
+    SY.dma_start(T.x[QR:PD, 0:D], T.land_o[1:ND]).then_inc(S.ld_xd, 16)
     SY.wait_ge(S.late_ml, 4)
-    SY.dma_start(T.mll[0:32, 0:2], T.land_ml[ND:16, r4:r4 + 4, :]).then_inc(S.ld_mll, 16)
+    SY.dma_start(T.ml_sb[PD:P, 0:2], T.land_ml[ND:NS, r4:r4 + 4, :]).then_inc(S.ld_mll, 16)
     SY.wait_ge(S.late_o, 4)
-    SY.dma_start(T.xl[0:32, 0:D], T.land_o[ND:16]).then_inc(S.ld_xl, 16)
+    SY.dma_start(T.x[PD:P, 0:D], T.land_o[ND:NS]).then_inc(S.ld_xl, 16)
 
+    V.wait_ge(s_mk, 1)
     V.wait_ge(S.own_ml, 16)
     V.wait_ge(S.ld_mld, 16)
-    V.wait_ge(s_mk, 1)
-    s_zd = mark(V.tensor_scalar(T.zd[0:PD, 0:ND], T.mask[0:PD, 0:ND], T.mld[0:PD, 0:1], None, mult))
-    V.wait_ge(s_nm0, 1)
-    V.wait_ge(s_nm1, 1)
-    s_gd = mark(V.tensor_scalar(T.gd[0:PD, 0:40], T.nm[0:PD, 0:40], T.mld[0:PD, 0:1], None, add))
-    s_ld = mark(V.tensor_copy(T.xd[0:PD, D:D + 1], T.mld[0:PD, 1:2]))
+    V.wait_ge(S.ld_mll, 16)
+    s_z = mark(V.tensor_scalar(T.z[0:P, 0:NS], T.mask[0:P, 0:NS], T.ml_sb[0:P, 0:1], None, mult))
+    V.wait_ge(s_nm, 1)
+    s_gm = mark(V.tensor_scalar(T.gm[0:P, 0:QR], T.nm[0:P, 0:QR], T.ml_sb[0:P, 0:1], None, add))
+    s_l = mark(V.tensor_copy(T.x[0:P, D:D + 1], T.ml_sb[0:P, 1:2]))
     PE.wait_ge(s_b, 1)
-    PE.wait_ge(s_zd, 1)
-    s_mf1 = mark(PE.matmul(T.p_mf1[0:PD, 0:ND], T.b[0:PD, 0:PD], T.zd[0:PD, 0:ND], True, True))
-    V.wait_ge(s_mf1, 1)
-    s_negm1 = mark(V.tensor_reduce(T.negm1[0:PD, 0:1], T.p_mf1[0:PD, 0:ND], AxisListType.X, mx, negate=True))
-    s_m1 = mark(V.tensor_reduce(T.mll[32:40, 0:1], T.p_mf1[32:40, 0:ND], AxisListType.X, mx))
-    ACT.wait_ge(s_gd, 1)
-    ACT.wait_ge(s_negm1, 1)
-    s_wd = mark(ACT.activation(T.wd[0:PD, 0:40], T.gd[0:PD, 0:40], ActivationFunctionType.Exp, bias=T.negm1[0:PD, 0:1]))
-    PE.wait_ge(s_wd, 1)
-    PE.wait_ge(s_ld, 1)
+    PE.wait_ge(s_z, 1)
+    s_mf = mark(PE.matmul(T.p_mf[0:P, 0:NS], T.b[0:P, 0:P], T.z[0:P, 0:NS], True, True))
+    V.wait_ge(s_mf, 1)
+    s_negm = mark(V.tensor_reduce(T.negm[0:P, 0:1], T.p_mf[0:P, 0:NS], AxisListType.X, mx, negate=True))
+    ACT.wait_ge(s_gm, 1)
+    ACT.wait_ge(s_negm, 1)
+    s_w = mark(ACT.activation(T.w[0:P, 0:QR], T.gm[0:P, 0:QR], Exp, bias=T.negm[0:P, 0:1]))
+    PE.wait_ge(s_w, 1)
+    PE.wait_ge(s_l, 1)
+    s_den = mark(PE.matmul(T.p_den[0:QR, 0:1], T.w[0:P, 0:QR], T.x[0:P, D:D + 1], True, True))
     PE.wait_ge(S.own_o, 16)
     PE.wait_ge(S.ld_xd, 16)
-    s_acc = mark(PE.matmul(T.p_acc[0:PL, 0:D + 1], T.wd[0:PD, 0:40], T.xd[0:PD, 0:D + 1], True, True))
-    ACT.wait_ge(s_acc, 1)
-    s_x5 = mark(ACT.activation(T.xl[32:40, 0:D + 1], T.p_acc[32:40, 0:D + 1], ActivationFunctionType.Copy))
-
-    V.wait_ge(S.ld_mll, 16)
-    V.wait_ge(s_m1, 1)
-    s_zl = mark(V.tensor_scalar(T.zl[0:PL, 0:5], T.mask[0:PL, 0:5], T.mll[0:PL, 0:1], None, mult))
-    s_gl = mark(V.tensor_scalar(T.gl[0:PL, 0:QR], T.nm[0:PL, 32:40], T.mll[0:PL, 0:1], None, add))
-    s_ll = mark(V.tensor_copy(T.xl[0:32, D:D + 1], T.mll[0:32, 1:2]))
-    PE.wait_ge(s_zl, 1)
-    s_mf2 = mark(PE.matmul(T.p_mf2[0:PL, 0:5], T.b[0:PL, 0:PL], T.zl[0:PL, 0:5], True, True))
-    V.wait_ge(s_mf2, 1)
-    s_negm = mark(V.tensor_reduce(T.negm[0:PL, 0:1], T.p_mf2[0:PL, 0:5], AxisListType.X, mx, negate=True))
-    ACT.wait_ge(s_gl, 1)
-    ACT.wait_ge(s_negm, 1)
-    s_wl = mark(ACT.activation(T.wl[0:PL, 0:QR], T.gl[0:PL, 0:QR], ActivationFunctionType.Exp, bias=T.negm[0:PL, 0:1]))
-    PE.wait_ge(s_wl, 1)
-    PE.wait_ge(s_x5, 1)
-    PE.wait_ge(s_ll, 1)
     PE.wait_ge(S.ld_xl, 16)
-    s_out = mark(PE.matmul(T.p_out[0:QR, 0:D + 1], T.wl[0:PL, 0:QR], T.xl[0:PL, 0:D + 1], True, True))
-    V.wait_ge(s_out, 1)
-    s_rd = mark(V.reciprocal(T.rden[0:QR, 0:1], T.p_out[0:QR, D:D + 1]))
+    s_out = mark(PE.matmul(T.p_out[0:QR, 0:D], T.w[0:P, 0:QR], T.x[0:P, 0:D], True, True))
+    V.wait_ge(s_den, 1)
+    s_rd = mark(V.reciprocal(T.rden[0:QR, 0:1], T.p_den[0:QR, 0:1]))
     V.wait_ge(s_rd, 1)
+    V.wait_ge(s_out, 1)
     s_y = mark(V.tensor_scalar(T.ysb[0:QR, 0:D], T.p_out[0:QR, 0:D], T.rden[0:QR, 0:1], None, mult))
     SY.wait_ge(s_y, 1)
     SY.dma_start(T.y[:], T.ysb[0:QR, 0:D]).then_inc(S.stored, 16)

@@ -3,6 +3,7 @@ from concourse.mybir import AluOpType, AxisListType, ActivationFunctionType
 
 QR = 8
 D = 128
+H = D // 2
 NS = 16
 ND = 12
 P = NS * QR
@@ -31,7 +32,8 @@ SCRATCH = {
     "p_b": ("psum", [128, 512], "float32"),
     "p_mf": ("psum", [128, 512], "float32"),
     "p_den": ("psum", [128, 512], "float32"),
-    "p_out": ("psum", [128, 512], "float32"),
+    "p_oa": ("psum", [128, 512], "float32"),
+    "p_ob": ("psum", [128, 512], "float32"),
 }
 SEMAPHORES = (["st_o", "st_ml", "own_o", "own_ml", "ld_mld", "ld_xd", "ld_mll", "ld_xl", "stored",
                "rin", "din_o", "late_o", "late_ml", "sent", "ml_h0", "ml_h1", "ml_h2", "ml_h3"]
@@ -91,10 +93,6 @@ def rank_program(g, core, T, topo):
     s_mk0 = mark(V.memset(T.mask[0:P, 0:NS], 1.0))
     g.wait_ge(s_ones, 1)
     s_st = mark(g.affine_select(T.st[0:QR, 0:P], T.ones[0:QR, 0:P], [[0, NS], [-1, QR]], AluOpType.is_equal, 0.0, 0, 1))
-    g.wait_ge(s_mk0, 1)
-    s_mk1 = mark(g.affine_select(T.mask[0:P, 0:NS], T.mask[0:P, 0:NS], [[-QR, NS]], AluOpType.is_ge, 0.0, 0, 1))
-    g.wait_ge(s_mk1, 1)
-    s_mk = mark(g.affine_select(T.mask[0:P, 0:NS], T.mask[0:P, 0:NS], [[QR, NS]], AluOpType.is_ge, 0.0, QR - 1, -1))
     PE.wait_ge(s_st, 1)
     s_pb = mark(PE.matmul(T.p_b[0:P, 0:P], T.st[0:QR, 0:P], T.st[0:QR, 0:P], True, True))
     V.wait_ge(s_pb, 1)
@@ -105,22 +103,26 @@ def rank_program(g, core, T, topo):
     mysem = S["ml_h%d" % topo.host(core)]
     relay_of = {d: [r for r in peer if topo.chip(r) == topo.chip(d) and topo.may_write(r, d)][0] for d in diag}
     ml_to = lambda ds: (T.stage_ml[:], [(d, T.land_ml[slot(d, core)]) for d in ds], mysem)
-    first = [ml_to([d]) for d in peer]
-    first += [(T.stage_o[T.rank_of(d)], [(relay_of[d], T.relay_o[slot(relay_of[d], core) - 4])], S.rin) for d in diag]
     rest = [ml_to(cable), ml_to(same)]
     rest += [(T.stage_o[T.rank_of(d)], [(d, T.land_o[slot(d, core)])], S.din_o) for d in cable + peer + same]
-    g.wait_ge(S.st_o, 16)
     g.wait_ge(S.st_ml, 32)
-    sent = fused(first)
+    sent = fused([ml_to([d]) for d in peer])
+    g.wait_ge(S.st_o, 16)
+    sent += fused([(T.stage_o[T.rank_of(d)], [(relay_of[d], T.relay_o[slot(relay_of[d], core) - 4])], S.rin) for d in diag])
     sent += fused(rest[0:8])
     sent += fused(rest[8:])
 
     nxt = [d for d in cable if topo.chip(d) == topo.chip(core)][0]
     peersem = S["ml_h%d" % topo.host(peer[0])]
-    g.wait_ge(S.rin, 4)
     g.wait_ge(peersem, 4)
-    sent += fused([(T.land_ml[4 + k], [(nxt, T.land_ml[slot(nxt, peer[k])])], S.late_ml) for k in range(4)]
-                  + [(T.relay_o[k], [(nxt, T.land_o[slot(nxt, peer[k])])], S.late_o) for k in range(4)])
+    sent += fused([(T.land_ml[4 + k], [(nxt, T.land_ml[slot(nxt, peer[k])])], S.late_ml) for k in range(4)])
+    g.wait_ge(S.rin, 4)
+    sent += fused([(T.relay_o[k], [(nxt, T.land_o[slot(nxt, peer[k])])], S.late_o) for k in range(4)])
+
+    g.wait_ge(s_mk0, 1)
+    s_mk1 = mark(g.affine_select(T.mask[0:P, 0:NS], T.mask[0:P, 0:NS], [[-QR, NS]], AluOpType.is_ge, 0.0, 0, 1))
+    g.wait_ge(s_mk1, 1)
+    s_mk = mark(g.affine_select(T.mask[0:P, 0:NS], T.mask[0:P, 0:NS], [[QR, NS]], AluOpType.is_ge, 0.0, QR - 1, -1))
 
     r4 = 4 * rank
     SY.wait_ge(mysem, len(same))
@@ -134,14 +136,14 @@ def rank_program(g, core, T, topo):
     SY.wait_ge(S.late_o, 4)
     SY.dma_start(T.x[PD:P, 0:D], T.land_o[ND:NS]).then_inc(S.ld_xl, 16)
 
+    for q in (V, ACT):
+        q.wait_ge(S.own_ml, 16)
+        q.wait_ge(S.ld_mld, 16)
+        q.wait_ge(S.ld_mll, 16)
     V.wait_ge(s_mk, 1)
-    V.wait_ge(S.own_ml, 16)
-    V.wait_ge(S.ld_mld, 16)
-    V.wait_ge(S.ld_mll, 16)
     s_z = mark(V.tensor_scalar(T.z[0:P, 0:NS], T.mask[0:P, 0:NS], T.ml_sb[0:P, 0:1], None, mult))
-    V.wait_ge(s_nm, 1)
-    s_gm = mark(V.tensor_scalar(T.gm[0:P, 0:QR], T.nm[0:P, 0:QR], T.ml_sb[0:P, 0:1], None, add))
-    s_l = mark(V.tensor_copy(T.x[0:P, D:D + 1], T.ml_sb[0:P, 1:2]))
+    s_gm = mark(ACT.activation(T.gm[0:P, 0:QR], T.nm[0:P, 0:QR], ActivationFunctionType.Identity, bias=T.ml_sb[0:P, 0:1]))
+    s_l = mark(ACT.activation(T.x[0:P, D:D + 1], T.ml_sb[0:P, 1:2], ActivationFunctionType.Copy))
     PE.wait_ge(s_b, 1)
     PE.wait_ge(s_z, 1)
     s_mf = mark(PE.matmul(T.p_mf[0:P, 0:NS], T.b[0:P, 0:P], T.z[0:P, 0:NS], True, True))
@@ -156,13 +158,18 @@ def rank_program(g, core, T, topo):
     PE.wait_ge(S.own_o, 16)
     PE.wait_ge(S.ld_xd, 16)
     PE.wait_ge(S.ld_xl, 16)
-    s_out = mark(PE.matmul(T.p_out[0:QR, 0:D], T.w[0:P, 0:QR], T.x[0:P, 0:D], True, True))
+    s_oa = mark(PE.matmul(T.p_oa[0:QR, 0:H], T.w[0:P, 0:QR], T.x[0:P, 0:H], True, True))
+    s_ob = mark(PE.matmul(T.p_ob[0:QR, 0:H], T.w[0:P, 0:QR], T.x[0:P, H:D], True, True))
     V.wait_ge(s_den, 1)
     s_rd = mark(V.reciprocal(T.rden[0:QR, 0:1], T.p_den[0:QR, 0:1]))
     V.wait_ge(s_rd, 1)
-    V.wait_ge(s_out, 1)
-    s_y = mark(V.tensor_scalar(T.ysb[0:QR, 0:D], T.p_out[0:QR, 0:D], T.rden[0:QR, 0:1], None, mult))
-    SY.wait_ge(s_y, 1)
+    V.wait_ge(s_oa, 1)
+    s_ya = mark(V.tensor_scalar(T.ysb[0:QR, 0:H], T.p_oa[0:QR, 0:H], T.rden[0:QR, 0:1], None, mult))
+    ACT.wait_ge(s_rd, 1)
+    ACT.wait_ge(s_ob, 1)
+    s_yb = mark(ACT.activation(T.ysb[0:QR, H:D], T.p_ob[0:QR, 0:H], ActivationFunctionType.Copy, scale=T.rden[0:QR, 0:1]))
+    SY.wait_ge(s_ya, 1)
+    SY.wait_ge(s_yb, 1)
     SY.dma_start(T.y[:], T.ysb[0:QR, 0:D]).then_inc(S.stored, 16)
 
     g.wait_ge(S.sent, sent)

@@ -8,13 +8,14 @@ NS = 16
 ND = 12
 P = NS * QR
 PD = ND * QR
+NE = 4
 BIG = 1.0e4
 
 SCRATCH = {
     "stage_o": ("dram", [16, 128, 8], "bfloat16"),
-    "stage_ml": ("dram", [128, 4], "float32"),
+    "stage_ml": ("dram", [128, 2], "float32"),
     "land_o": ("dram", [16, 128, 8], "bfloat16"),
-    "land_ml": ("dram", [16, 128, 4], "float32"),
+    "land_ml": ("dram", [16, 128, 2], "float32"),
     "relay_o": ("dram", [4, 128, 8], "bfloat16"),
     "x": ("sbuf", [128, 136], "bfloat16"),
     "ml_sb": ("sbuf", [128, 2], "float32"),
@@ -83,11 +84,11 @@ def rank_program(g, core, T, topo):
                             for i, (src, dl, sem) in enumerate(items)], local_sem=S.sent)
         return len(items)
 
-    SY.dma_start(T.stage_o[:], T.o[:]).then_inc(S.st_o, 16)
-    ACT.dma_start(T.stage_ml[0:64, :], T.ml[:]).then_inc(S.st_ml, 16)
-    ACT.dma_start(T.stage_ml[64:128, :], T.ml[:]).then_inc(S.st_ml, 16)
+    ACT.dma_start(T.stage_ml[:], T.ml[:]).then_inc(S.st_ml, 16)
+    ACT.dma_start(T.stage_o[:], T.o[:]).then_inc(S.st_o, 16)
+    SY.wait_ge(S.st_o, 16)
+    SY.dma_start(T.ml_sb[0:QR, 0:2], T.ml[QR * rank:QR * rank + QR, :]).then_inc(S.own_ml, 16)
     SY.dma_start(T.x[0:QR, 0:D], T.o[QR * rank:QR * rank + QR, :]).then_inc(S.own_o, 16)
-    ACT.dma_start(T.ml_sb[0:QR, 0:2], T.ml[QR * rank:QR * rank + QR, :]).then_inc(S.own_ml, 16)
 
     s_ones = mark(V.memset(T.ones[0:QR, 0:P], 1.0))
     s_mk0 = mark(V.memset(T.mask[0:P, 0:NS], 1.0))
@@ -103,14 +104,14 @@ def rank_program(g, core, T, topo):
     mysem = S["ml_h%d" % topo.host(core)]
     relay_of = {d: [r for r in peer if topo.chip(r) == topo.chip(d) and topo.may_write(r, d)][0] for d in diag}
     ml_to = lambda ds: (T.stage_ml[:], [(d, T.land_ml[slot(d, core)]) for d in ds], mysem)
-    rest = [ml_to(cable), ml_to(same)]
-    rest += [(T.stage_o[T.rank_of(d)], [(d, T.land_o[slot(d, core)])], S.din_o) for d in cable + peer + same]
-    g.wait_ge(S.st_ml, 32)
-    sent = fused([ml_to([d]) for d in peer])
+    others = cable + same
+    direct = [(T.stage_o[T.rank_of(d)], [(d, T.land_o[slot(d, core)])], S.din_o) for d in cable + peer + same]
+    g.wait_ge(S.st_ml, 16)
+    sent = fused([ml_to([peer[i]] + others[i::NE]) for i in range(NE)])
     g.wait_ge(S.st_o, 16)
     sent += fused([(T.stage_o[T.rank_of(d)], [(relay_of[d], T.relay_o[slot(relay_of[d], core) - 4])], S.rin) for d in diag])
-    sent += fused(rest[0:8])
-    sent += fused(rest[8:])
+    for i in range(0, len(direct), NE):
+        sent += fused(direct[i:i + NE])
 
     nxt = [d for d in cable if topo.chip(d) == topo.chip(core)][0]
     peersem = S["ml_h%d" % topo.host(peer[0])]
@@ -124,15 +125,15 @@ def rank_program(g, core, T, topo):
     g.wait_ge(s_mk1, 1)
     s_mk = mark(g.affine_select(T.mask[0:P, 0:NS], T.mask[0:P, 0:NS], [[QR, NS]], AluOpType.is_ge, 0.0, QR - 1, -1))
 
-    r4 = 4 * rank
+    q0 = QR * rank
     SY.wait_ge(mysem, len(same))
     SY.wait_ge(peersem, 4)
     SY.wait_ge(S["ml_h%d" % topo.host(cable[0])], 4)
-    SY.dma_start(T.ml_sb[QR:PD, 0:2], T.land_ml[1:ND, r4:r4 + 4, :]).then_inc(S.ld_mld, 16)
-    SY.wait_ge(S.din_o, ND - 1)
-    SY.dma_start(T.x[QR:PD, 0:D], T.land_o[1:ND]).then_inc(S.ld_xd, 16)
+    SY.dma_start(T.ml_sb[QR:PD, 0:2], T.land_ml[1:ND, q0:q0 + QR, :]).then_inc(S.ld_mld, 16)
+    ACT.wait_ge(S.din_o, ND - 1)
+    ACT.dma_start(T.x[QR:PD, 0:D], T.land_o[1:ND]).then_inc(S.ld_xd, 16)
     SY.wait_ge(S.late_ml, 4)
-    SY.dma_start(T.ml_sb[PD:P, 0:2], T.land_ml[ND:NS, r4:r4 + 4, :]).then_inc(S.ld_mll, 16)
+    SY.dma_start(T.ml_sb[PD:P, 0:2], T.land_ml[ND:NS, q0:q0 + QR, :]).then_inc(S.ld_mll, 16)
     SY.wait_ge(S.late_o, 4)
     SY.dma_start(T.x[PD:P, 0:D], T.land_o[ND:NS]).then_inc(S.ld_xl, 16)
 

from concourse.bass import DstId, RemoteDMATransfer
from concourse.mybir import AluOpType, AxisListType, ActivationFunctionType

QR = 8
D = 128
H = D // 2
NS = 16
ND = 12
P = NS * QR
PD = ND * QR
NE = 4
BIG = 1.0e4

SCRATCH = {
    "stage_o": ("dram", [16, 128, 8], "bfloat16"),
    "stage_ml": ("dram", [128, 2], "float32"),
    "land_o": ("dram", [16, 128, 8], "bfloat16"),
    "land_ml": ("dram", [16, 128, 2], "float32"),
    "relay_o": ("dram", [4, 128, 8], "bfloat16"),
    "x": ("sbuf", [128, 136], "bfloat16"),
    "ml_sb": ("sbuf", [128, 2], "float32"),
    "ones": ("sbuf", [128, P], "float32"),
    "st": ("sbuf", [128, P], "float32"),
    "b": ("sbuf", [128, P], "bfloat16"),
    "mask": ("sbuf", [128, NS], "float32"),
    "nm": ("sbuf", [128, QR], "float32"),
    "z": ("sbuf", [128, NS], "bfloat16"),
    "gm": ("sbuf", [128, QR], "float32"),
    "w": ("sbuf", [128, QR], "bfloat16"),
    "negm": ("sbuf", [128, 1], "float32"),
    "rden": ("sbuf", [128, 1], "float32"),
    "ysb": ("sbuf", [128, D], "bfloat16"),
    "p_b": ("psum", [128, 512], "float32"),
    "p_mf": ("psum", [128, 512], "float32"),
    "p_den": ("psum", [128, 512], "float32"),
    "p_oa": ("psum", [128, 512], "float32"),
    "p_ob": ("psum", [128, 512], "float32"),
}
SEMAPHORES = (["st_o", "st_ml", "own_o", "own_ml", "ld_mld", "ld_xd", "ld_mll", "ld_xl", "stored",
               "rin", "din_o", "late_o", "late_ml", "sent", "ml_h0", "ml_h1", "ml_h2", "ml_h3"]
              + ["c%d" % i for i in range(24)])


def _order(d, cores, topo):
    same = [c for c in cores if c != d and topo.host(c) == topo.host(d)]
    peer = [c for c in cores if topo.host(c) != topo.host(d) and topo.rack(topo.host(c)) == topo.rack(topo.host(d))]
    far = [c for c in cores if topo.rack(topo.host(c)) != topo.rack(topo.host(d))]
    cable = [c for c in far if topo.may_write(c, d)]
    diag = [c for c in far if not topo.may_write(c, d)]
    return [d] + same + peer + cable + diag, same, peer, cable, diag


def rank_program(g, core, T, topo):
    rank = T.rank_of(core)
    if rank is None:
        return
    cores = list(T.cores)
    S = T.sem
    V, PE, ACT, SY = g.vector, g.tensor, g.scalar, g.sync
    mult, add, mx = AluOpType.mult, AluOpType.add, AluOpType.max
    Exp = ActivationFunctionType.Exp
    _, same, peer, cable, diag = _order(core, cores, topo)
    slot = lambda dst, src: _order(dst, cores, topo)[0].index(src)
    nsem = [0]

    def mark(ins):
        s = S["c%d" % nsem[0]]
        nsem[0] += 1
        ins.then_inc(s, 1)
        return s

    def did(dst):
        rid, pid = topo.addr(dst, core)
        return DstId(rid=rid, pnc=pid)

    def fused(items):
        ok = ~0
        for _, dl, _ in items:
            for dst, _ in dl:
                ok &= topo.mask(core, dst)
        eng = [1 << i for i in range(16) if (ok >> i) & 1]
        g.remote_dma_fused([RemoteDMATransfer(dst_ids=[did(dst) for dst, _ in dl], dma_engine_mask=eng[i], remote_sem=sem,
                                              srcs=[src], dsts=[ap for _, ap in dl])
                            for i, (src, dl, sem) in enumerate(items)], local_sem=S.sent)
        return len(items)

    ACT.dma_start(T.stage_ml[:], T.ml[:]).then_inc(S.st_ml, 16)
    ACT.dma_start(T.stage_o[:], T.o[:]).then_inc(S.st_o, 16)
    SY.wait_ge(S.st_o, 16)
    SY.dma_start(T.ml_sb[0:QR, 0:2], T.ml[QR * rank:QR * rank + QR, :]).then_inc(S.own_ml, 16)
    SY.dma_start(T.x[0:QR, 0:D], T.o[QR * rank:QR * rank + QR, :]).then_inc(S.own_o, 16)

    s_ones = mark(V.memset(T.ones[0:QR, 0:P], 1.0))
    s_mk0 = mark(V.memset(T.mask[0:P, 0:NS], 1.0))
    g.wait_ge(s_ones, 1)
    s_st = mark(g.affine_select(T.st[0:QR, 0:P], T.ones[0:QR, 0:P], [[0, NS], [-1, QR]], AluOpType.is_equal, 0.0, 0, 1))
    PE.wait_ge(s_st, 1)
    s_pb = mark(PE.matmul(T.p_b[0:P, 0:P], T.st[0:QR, 0:P], T.st[0:QR, 0:P], True, True))
    V.wait_ge(s_pb, 1)
    s_nm = mark(V.tensor_scalar(T.nm[0:P, 0:QR], T.p_b[0:P, 0:QR], -1.0, BIG, add, mult))
    ACT.wait_ge(s_nm, 1)
    s_b = mark(ACT.activation(T.b[0:P, 0:P], T.p_b[0:P, 0:P], Exp, bias=-BIG, scale=BIG))

    mysem = S["ml_h%d" % topo.host(core)]
    relay_of = {d: [r for r in peer if topo.chip(r) == topo.chip(d) and topo.may_write(r, d)][0] for d in diag}
    ml_to = lambda ds: (T.stage_ml[:], [(d, T.land_ml[slot(d, core)]) for d in ds], mysem)
    others = cable + same
    direct = [(T.stage_o[T.rank_of(d)], [(d, T.land_o[slot(d, core)])], S.din_o) for d in cable + peer + same]
    g.wait_ge(S.st_ml, 16)
    sent = fused([ml_to([peer[i]] + others[i::NE]) for i in range(NE)])
    g.wait_ge(S.st_o, 16)
    sent += fused([(T.stage_o[T.rank_of(d)], [(relay_of[d], T.relay_o[slot(relay_of[d], core) - 4])], S.rin) for d in diag])
    for i in range(0, len(direct), NE):
        sent += fused(direct[i:i + NE])

    nxt = [d for d in cable if topo.chip(d) == topo.chip(core)][0]
    peersem = S["ml_h%d" % topo.host(peer[0])]
    g.wait_ge(peersem, 4)
    sent += fused([(T.land_ml[4 + k], [(nxt, T.land_ml[slot(nxt, peer[k])])], S.late_ml) for k in range(4)])
    g.wait_ge(S.rin, 4)
    sent += fused([(T.relay_o[k], [(nxt, T.land_o[slot(nxt, peer[k])])], S.late_o) for k in range(4)])

    g.wait_ge(s_mk0, 1)
    s_mk1 = mark(g.affine_select(T.mask[0:P, 0:NS], T.mask[0:P, 0:NS], [[-QR, NS]], AluOpType.is_ge, 0.0, 0, 1))
    g.wait_ge(s_mk1, 1)
    s_mk = mark(g.affine_select(T.mask[0:P, 0:NS], T.mask[0:P, 0:NS], [[QR, NS]], AluOpType.is_ge, 0.0, QR - 1, -1))

    q0 = QR * rank
    SY.wait_ge(mysem, len(same))
    SY.wait_ge(peersem, 4)
    SY.wait_ge(S["ml_h%d" % topo.host(cable[0])], 4)
    SY.dma_start(T.ml_sb[QR:PD, 0:2], T.land_ml[1:ND, q0:q0 + QR, :]).then_inc(S.ld_mld, 16)
    ACT.wait_ge(S.din_o, ND - 1)
    ACT.dma_start(T.x[QR:PD, 0:D], T.land_o[1:ND]).then_inc(S.ld_xd, 16)
    SY.wait_ge(S.late_ml, 4)
    SY.dma_start(T.ml_sb[PD:P, 0:2], T.land_ml[ND:NS, q0:q0 + QR, :]).then_inc(S.ld_mll, 16)
    SY.wait_ge(S.late_o, 4)
    SY.dma_start(T.x[PD:P, 0:D], T.land_o[ND:NS]).then_inc(S.ld_xl, 16)

    for q in (V, ACT):
        q.wait_ge(S.own_ml, 16)
        q.wait_ge(S.ld_mld, 16)
        q.wait_ge(S.ld_mll, 16)
    V.wait_ge(s_mk, 1)
    s_z = mark(V.tensor_scalar(T.z[0:P, 0:NS], T.mask[0:P, 0:NS], T.ml_sb[0:P, 0:1], None, mult))
    s_gm = mark(ACT.activation(T.gm[0:P, 0:QR], T.nm[0:P, 0:QR], ActivationFunctionType.Identity, bias=T.ml_sb[0:P, 0:1]))
    s_l = mark(ACT.activation(T.x[0:P, D:D + 1], T.ml_sb[0:P, 1:2], ActivationFunctionType.Copy))
    PE.wait_ge(s_b, 1)
    PE.wait_ge(s_z, 1)
    s_mf = mark(PE.matmul(T.p_mf[0:P, 0:NS], T.b[0:P, 0:P], T.z[0:P, 0:NS], True, True))
    V.wait_ge(s_mf, 1)
    s_negm = mark(V.tensor_reduce(T.negm[0:P, 0:1], T.p_mf[0:P, 0:NS], AxisListType.X, mx, negate=True))
    ACT.wait_ge(s_gm, 1)
    ACT.wait_ge(s_negm, 1)
    s_w = mark(ACT.activation(T.w[0:P, 0:QR], T.gm[0:P, 0:QR], Exp, bias=T.negm[0:P, 0:1]))
    PE.wait_ge(s_w, 1)
    PE.wait_ge(s_l, 1)
    s_den = mark(PE.matmul(T.p_den[0:QR, 0:1], T.w[0:P, 0:QR], T.x[0:P, D:D + 1], True, True))
    PE.wait_ge(S.own_o, 16)
    PE.wait_ge(S.ld_xd, 16)
    PE.wait_ge(S.ld_xl, 16)
    s_oa = mark(PE.matmul(T.p_oa[0:QR, 0:H], T.w[0:P, 0:QR], T.x[0:P, 0:H], True, True))
    s_ob = mark(PE.matmul(T.p_ob[0:QR, 0:H], T.w[0:P, 0:QR], T.x[0:P, H:D], True, True))
    V.wait_ge(s_den, 1)
    s_rd = mark(V.reciprocal(T.rden[0:QR, 0:1], T.p_den[0:QR, 0:1]))
    V.wait_ge(s_rd, 1)
    V.wait_ge(s_oa, 1)
    s_ya = mark(V.tensor_scalar(T.ysb[0:QR, 0:H], T.p_oa[0:QR, 0:H], T.rden[0:QR, 0:1], None, mult))
    ACT.wait_ge(s_rd, 1)
    ACT.wait_ge(s_ob, 1)
    s_yb = mark(ACT.activation(T.ysb[0:QR, H:D], T.p_ob[0:QR, 0:H], ActivationFunctionType.Copy, scale=T.rden[0:QR, 0:1]))
    SY.wait_ge(s_ya, 1)
    SY.wait_ge(s_yb, 1)
    SY.dma_start(T.y[:], T.ysb[0:QR, 0:D]).then_inc(S.stored, 16)

    g.wait_ge(S.sent, sent)
    g.wait_ge(S.stored, 16)
